import numpy as np
import ml_dtypes


def mxq(x, axis, fmt="e4m3"):
    dtype, down = {"e4m3": (ml_dtypes.float8_e4m3fn, 7), "e5m2": (ml_dtypes.float8_e5m2, 14)}[fmt]
    v = np.moveaxis(np.asarray(x, np.float32).astype(ml_dtypes.bfloat16).astype(np.float64), axis, -1)
    blocks = v.reshape(v.shape[:-1] + (-1, 32))
    amax = np.abs(blocks).max(-1, keepdims=True)
    byte = np.maximum(np.where(amax > 0, np.frexp(amax)[1] - 1 + 127, 0) - down, 1)
    scale = np.exp2(byte - 127.0)
    codes = (blocks / scale).astype(np.float32).astype(dtype).astype(np.float64)
    return np.moveaxis((codes * scale).reshape(v.shape), -1, axis)


WIDE = False


def mx_kscale(k):
    if not WIDE:
        return np.ones(k)
    levels = np.array([10, -10, 5, -5, 0])
    if k % 512:
        return np.exp2(np.random.permutation(np.resize(levels, k // 32))).repeat(32)
    a = np.empty((k // 512, 16))
    for p in range(k // 512):
        a[p, :8] = np.random.permutation(np.resize(levels, 8))
        for g in range(8):
            far = levels[np.abs(levels - a[p, g]) >= 10]
            a[p, g + 8] = far[np.random.randint(len(far))]
    return np.exp2(a.ravel()).repeat(32)


def f64(x):
    return np.asarray(x).astype(np.float64)


def striped(idx):
    return np.tile(idx.reshape(-1, 16).T, (8, 1)).astype(np.uint16)


def unstriped(offs):
    return offs[:16].T.reshape(-1).astype(np.int64)


def pack_weight(w):
    k, n = w.shape
    w = f64(np.asarray(w, np.float32).astype(ml_dtypes.bfloat16)).reshape(k // 32, 32, n)
    amax = np.abs(w).max(1)
    byte = np.clip(np.where(amax > 0, np.frexp(amax)[1] - 1 + 127 - 7, 1), 1, 254)
    scaled = (w * np.exp2(127.0 - byte)[:, None, :]).reshape(k, n).astype(np.float32)
    words = np.ascontiguousarray(scaled.reshape(k // 512, 128, 4, n).transpose(0, 1, 3, 2)).astype(ml_dtypes.float8_e4m3fn).view(np.uint8)
    return words, np.ascontiguousarray(byte.astype(np.uint8).reshape(k // 512, 16, n))


def unpack_weight(words, scales):
    g, p, n, _ = words.shape
    vals = np.ascontiguousarray(words).view(ml_dtypes.float8_e4m3fn).astype(np.float64) * np.repeat(np.exp2(scales.astype(np.float64) - 127.0), 8, axis=1)[..., None]
    return vals.transpose(0, 1, 3, 2).reshape(g * 512, n)


K, T, S, N, H = 512, 1024, 512, 256, 512


def setup_inputs():
    n = np.random.standard_normal
    s = mx_kscale(K)[:, None]
    u = mx_kscale(H)
    packed_xT = pack_weight(n((K, T)) * s)
    return {
        "x_words": packed_xT[0],
        "x_scales": packed_xT[1],
        "w1": (n((K, H)) / np.sqrt(K) / s).astype(np.float32),
        "unit": (np.random.uniform(0.6, 1.4, (H, 1)) * u[:, None]).astype(np.float32),
        "w2": (n((H, N)) / np.sqrt(H) / u[:, None]).astype(np.float32),
        "offs": striped(np.random.permutation(T)[:S]),
        "h1": striped(np.random.permutation(S)),
        "h2": striped(np.random.permutation(S)),
        "h3": striped(np.random.permutation(S)),
    }


def reference(x_words, x_scales, w1, unit, w2, offs, h1, h2, h3):
    xq = unpack_weight(x_words, x_scales)[:, unstriped(offs)]
    uu = mxq(f64(w1), 0, "e4m3").T @ xq
    heat = np.exp(0.8 * np.tanh(uu))
    a1 = heat[:, unstriped(h1)]
    gx = a1 - heat
    a2 = heat[:, unstriped(h2)]
    gy = a2 - heat
    nrm = np.sqrt((gx) ** 2 + (gy) ** 2 + 0.05)
    vx = gx / nrm
    xb = vx[:, unstriped(h3)]
    vy = gy / nrm
    yb = vy[:, unstriped(h3)]
    div_ = vx - xb + vy - yb
    hid = f64(unit) * div_
    return mxq(f64(w2), 0, "e4m3").T @ mxq(hid, 0, "e4m3")

@@ -1,0 +1,143 @@
+from contextlib import ExitStack
+
+import concourse.mybir as mybir
+
+K, T, S, N, H = 512, 1024, 512, 256, 512
+FLOPS = 2 * K * H * S + 2 * H * N * S
+
+F32 = mybir.dt.float32
+BF16 = mybir.dt.bfloat16
+I32 = mybir.dt.int32
+U32 = mybir.dt.uint32
+U16 = mybir.dt.uint16
+U8 = mybir.dt.uint8
+FP8X4 = mybir.dt.float8_e4m3fn_x4
+ACT = mybir.ActivationFunctionType
+ALU = mybir.AluOpType
+
+P = 128
+PACK = 4
+CHUNKS = ((0, 256), (256, 128), (384, 128))
+
+
+def tile_picked_yheatg_div_p_kernel(tc, x_words, x_scales, w1, unit, w2, offs, h1, h2, h3, out):
+    nc = tc.nc
+    with ExitStack() as ctx:
+        keep = ctx.enter_context(tc.tile_pool(name="keep", bufs=1))
+        psum = ctx.enter_context(tc.psum_pool(name="psum", bufs=1))
+
+        offs_t = keep.tile([P, S // 16], U16, name="offs_t")
+        nc.sync.dma_start(offs_t[:], offs)
+        words = keep.tile([P, T], U32, name="words")
+        nc.sync.dma_start(words[:].bitcast(I32), x_words[0].rearrange("p n r -> p (n r)").bitcast(I32))
+        scales = keep.tile([P, T], U8, name="scales")
+        for q in range(4):
+            nc.scalar.dma_start(scales[32 * q : 32 * q + 32, :].bitcast(I32), x_scales[0, 4 * q : 4 * q + 4, :].bitcast(I32).partition_broadcast(8))
+        w1_raw = keep.tile([P, PACK, H], F32, name="w1_raw")
+        nc.sync.dma_start(w1_raw[:], w1.rearrange("(p j) c -> p j c", j=PACK))
+        w2_raw = keep.tile([P, PACK, N], F32, name="w2_raw")
+        nc.sync.dma_start(w2_raw[:], w2.rearrange("(p j) c -> p j c", j=PACK))
+        lists = []
+        for name, src in (("h1_t", h1), ("h2_t", h2), ("h3_t", h3)):
+            lst = keep.tile([P, S // 16], U16, name=name)
+            nc.sync.dma_start(lst[:], src)
+            lists.append(lst)
+        h1_t, h2_t, h3_t = lists
+        unit_t = keep.tile([P, PACK], F32, name="unit_t")
+        nc.sync.dma_start(unit_t[:], unit.rearrange("(p t) o -> p (t o)", t=PACK))
+
+        x_codes = keep.tile([P, S], U32, name="x_codes", align_bytes=64)
+        x_bytes = keep.tile([P, S], U8, name="x_bytes", align_bytes=64)
+        nc.vector.tensor_copy(x_codes[:], words[:].indirect(offs_t[:]))
+        nc.vector.tensor_copy(x_bytes[:], scales[:].indirect(offs_t[:]))
+
+        dealt = w1_raw[:].rearrange("p j (m t) -> p m t j", t=PACK)
+        w1_bf = [keep.tile([P, P, PACK], BF16, name=f"w1_bf{t}", align_bytes=64) for t in range(2)]
+        w1_bf23 = keep.tile([P, 2, P, PACK], BF16, name="w1_bf23", align_bytes=64)
+        w1_codes = [keep.tile([P, P], U32, name=f"w1_codes{t}", align_bytes=64) for t in range(PACK)]
+        w1_bytes = [keep.tile([P, P], U8, name=f"w1_bytes{t}", align_bytes=64) for t in range(PACK)]
+        uu = [psum.tile([P, S], F32, name=f"uu{t}") for t in range(PACK)]
+        heat = [keep.tile([P, 2 * S], F32, name=f"heat{t}") for t in range(PACK)]
+        heat_copy = [keep.tile([P, S], F32, name=f"heat_copy{t}") for t in range(PACK)]
+
+        nc.vector.tensor_copy(w1_bf[0][:], dealt[:, :, 0, :])
+        nc.scalar.copy(w1_bf[1][:], dealt[:, :, 1, :])
+        sources = [w1_bf[0][:], w1_bf[1][:], w1_bf23[:, 0], w1_bf23[:, 1]]
+        for t in range(PACK):
+            if t == 1:
+                nc.vector.tensor_copy(w1_bf23[:].rearrange("p t m j -> p m t j"), dealt[:, :, 2:4, :])
+            nc.vector.quantize_mx(out=w1_codes[t][:].bitcast(FP8X4), scales=w1_bytes[t][:], in_=sources[t].rearrange("p m j -> p (m j)"))
+            nc.tensor.matmul_mx(out=uu[t][:], lhsT=w1_codes[t][:].bitcast(FP8X4), lhsT_scale=w1_bytes[t][:],
+                                rhs=x_codes[:].bitcast(FP8X4), rhs_scale=x_bytes[:], start=True, stop=True)
+            nc.scalar.activation(heat[t][:, S:], uu[t][:], ACT.Tanh)
+            nc.scalar.activation(heat[t][:, :S], heat[t][:, S:], ACT.Exp, scale=0.8)
+
+        w2_bf = keep.tile([P, N, PACK], BF16, name="w2_bf", align_bytes=64)
+        w2_codes = keep.tile([P, N], U32, name="w2_codes", align_bytes=64)
+        w2_bytes = keep.tile([P, N], U8, name="w2_bytes", align_bytes=64)
+        nc.vector.tensor_copy(w2_bf[:], w2_raw[:].rearrange("p j c -> p c j"))
+        nc.vector.quantize_mx(out=w2_codes[:].bitcast(FP8X4), scales=w2_bytes[:], in_=w2_bf[:].rearrange("p c j -> p (c j)"))
+
+        grad = [keep.tile([P, 2 * S], F32, name=f"grad{t}") for t in range(PACK)]
+        sq = [keep.tile([P, 2 * S], F32, name=f"sq{t}") for t in range(PACK)]
+        gsum = [keep.tile([P, S], F32, name=f"gsum{t}") for t in range(PACK)]
+        qq = [keep.tile([P, S], F32, name=f"qq{t}") for t in range(PACK)]
+        field = keep.tile([P, PACK, 2 * S], F32, name="field")
+        fetched = keep.tile([P, PACK, S], F32, name="fetched")
+
+        def edges(t):
+            if t < 2:
+                nc.vector.tensor_copy(heat_copy[t][:], heat[t][:, :S])
+            else:
+                nc.sync.dma_start(heat_copy[t][:], heat[t][:, :S])
+            nc.vector.tensor_tensor(grad[t][:, :S], heat[t][:].indirect(h1_t[:]), heat_copy[t][:], ALU.subtract)
+            nc.vector.tensor_tensor(grad[t][:, S:], heat[t][:].indirect(h2_t[:]), heat_copy[t][:], ALU.subtract)
+            nc.scalar.activation(sq[t][:], grad[t][:], ACT.Square)
+
+        def norm(t):
+            nc.vector.tensor_tensor(gsum[t][:], grad[t][:, :S], grad[t][:, S:], ALU.add)
+            nc.vector.tensor_tensor(qq[t][:], sq[t][:, :S], sq[t][:, S:], ALU.add)
+            nc.scalar.activation(field[:, t, S:], qq[t][:], ACT.Abs_reciprocal_sqrt, bias=0.05)
+
+        def unit_field(t):
+            nc.vector.scalar_tensor_tensor(field[:, t, :S], gsum[t][:], unit_t[:, t : t + 1], field[:, t, S:], ALU.mult, ALU.mult)
+
+        def fetch(t, c0, n):
+            nc.scalar.activation(fetched[:, t, c0 : c0 + n], field[:, t, :].indirect(h3_t[:, c0 // 16 : (c0 + n) // 16]), ACT.Copy)
+
+        edges(0)
+        edges(1)
+        norm(0)
+        edges(2)
+        norm(1)
+        unit_field(0)
+        fetch(0, 0, S)
+        edges(3)
+        norm(2)
+        unit_field(1)
+        fetch(1, 0, S)
+        norm(3)
+        unit_field(2)
+        fetch(2, 0, S)
+        unit_field(3)
+
+        out_view = out.rearrange("(g p) j -> p g j", p=P)
+        for c0, n in CHUNKS:
+            fetch(3, c0, n)
+            hid = keep.tile([P, n * PACK], BF16, name=f"hid{c0}", align_bytes=64)
+            nc.vector.tensor_tensor(
+                hid[:].rearrange("p (c i t) -> p c t i", i=4, t=PACK),
+                field[:, :, c0 : c0 + n].rearrange("p t (c i) -> p c t i", i=4),
+                fetched[:, :, c0 : c0 + n].rearrange("p t (c i) -> p c t i", i=4),
+                ALU.subtract,
+            )
+            hid_codes = keep.tile([P, n], U32, name=f"hid_codes{c0}", align_bytes=64)
+            hid_bytes = keep.tile([P, n], U8, name=f"hid_bytes{c0}", align_bytes=64)
+            nc.vector.quantize_mx(out=hid_codes[:].bitcast(FP8X4), scales=hid_bytes[:], in_=hid[:])
+            acc = psum.tile([P, 2, n], F32, name=f"acc{c0}")
+            for g in range(2):
+                nc.tensor.matmul_mx(out=acc[:, g, :], lhsT=w2_codes[:, g * P : (g + 1) * P].bitcast(FP8X4), lhsT_scale=w2_bytes[:, g * P : (g + 1) * P],
+                                    rhs=hid_codes[:].bitcast(FP8X4), rhs_scale=hid_bytes[:], start=True, stop=True)
+            staged = keep.tile([P, 2, n], F32, name=f"staged{c0}")
+            nc.scalar.copy(staged[:], acc[:])
+            nc.sync.dma_start(out_view[:, :, c0 : c0 + n], staged[:])

@@ -1,6 +1,7 @@
 from contextlib import ExitStack
 
 import concourse.mybir as mybir
+from concourse.masks import make_identity
 
 K, T, S, N, H = 512, 1024, 512, 256, 512
 FLOPS = 2 * K * H * S + 2 * H * N * S
@@ -17,7 +18,8 @@ ALU = mybir.AluOpType
 
 P = 128
 PACK = 4
-CHUNKS = ((0, 256), (256, 128), (384, 128))
+HALF = S // 2
+CHUNKS = ((0, 128), (128, 128), (256, 128), (384, 128))
 
 
 def tile_picked_yheatg_div_p_kernel(tc, x_words, x_scales, w1, unit, w2, offs, h1, h2, h3, out):
@@ -26,13 +28,16 @@ def tile_picked_yheatg_div_p_kernel(tc, x_words, x_scales, w1, unit, w2, offs, h
         keep = ctx.enter_context(tc.tile_pool(name="keep", bufs=1))
         psum = ctx.enter_context(tc.psum_pool(name="psum", bufs=1))
 
+        def bank(number, shape, name):
+            return psum.tile(shape, F32, name=name, tag=f"bank{number}")
+
         offs_t = keep.tile([P, S // 16], U16, name="offs_t")
         nc.sync.dma_start(offs_t[:], offs)
         words = keep.tile([P, T], U32, name="words")
         nc.sync.dma_start(words[:].bitcast(I32), x_words[0].rearrange("p n r -> p (n r)").bitcast(I32))
         scales = keep.tile([P, T], U8, name="scales")
         for q in range(4):
-            nc.scalar.dma_start(scales[32 * q : 32 * q + 32, :].bitcast(I32), x_scales[0, 4 * q : 4 * q + 4, :].bitcast(I32).partition_broadcast(8))
+            (nc.scalar if q < 2 else nc.sync).dma_start(scales[32 * q : 32 * q + 32, :].bitcast(I32), x_scales[0, 4 * q : 4 * q + 4, :].bitcast(I32).partition_broadcast(8))
         w1_raw = keep.tile([P, PACK, H], F32, name="w1_raw")
         nc.sync.dma_start(w1_raw[:], w1.rearrange("(p j) c -> p j c", j=PACK))
         w2_raw = keep.tile([P, PACK, N], F32, name="w2_raw")
@@ -45,6 +50,8 @@ def tile_picked_yheatg_div_p_kernel(tc, x_words, x_scales, w1, unit, w2, offs, h
         h1_t, h2_t, h3_t = lists
         unit_t = keep.tile([P, PACK], F32, name="unit_t")
         nc.sync.dma_start(unit_t[:], unit.rearrange("(p t) o -> p (t o)", t=PACK))
+        ident = keep.tile([P, P], F32, name="ident")
+        make_identity(nc, ident[:])
 
         x_codes = keep.tile([P, S], U32, name="x_codes", align_bytes=64)
         x_bytes = keep.tile([P, S], U8, name="x_bytes", align_bytes=64)
@@ -52,25 +59,24 @@ def tile_picked_yheatg_div_p_kernel(tc, x_words, x_scales, w1, unit, w2, offs, h
         nc.vector.tensor_copy(x_bytes[:], scales[:].indirect(offs_t[:]))
 
         dealt = w1_raw[:].rearrange("p j (m t) -> p m t j", t=PACK)
-        w1_bf = [keep.tile([P, P, PACK], BF16, name=f"w1_bf{t}", align_bytes=64) for t in range(2)]
-        w1_bf23 = keep.tile([P, 2, P, PACK], BF16, name="w1_bf23", align_bytes=64)
+        w1_bf = [keep.tile([P, 2, P, PACK], BF16, name=f"w1_bf{u}", align_bytes=64) for u in range(2)]
         w1_codes = [keep.tile([P, P], U32, name=f"w1_codes{t}", align_bytes=64) for t in range(PACK)]
         w1_bytes = [keep.tile([P, P], U8, name=f"w1_bytes{t}", align_bytes=64) for t in range(PACK)]
-        uu = [psum.tile([P, S], F32, name=f"uu{t}") for t in range(PACK)]
         heat = [keep.tile([P, 2 * S], F32, name=f"heat{t}") for t in range(PACK)]
         heat_copy = [keep.tile([P, S], F32, name=f"heat_copy{t}") for t in range(PACK)]
 
-        nc.vector.tensor_copy(w1_bf[0][:], dealt[:, :, 0, :])
-        nc.scalar.copy(w1_bf[1][:], dealt[:, :, 1, :])
-        sources = [w1_bf[0][:], w1_bf[1][:], w1_bf23[:, 0], w1_bf23[:, 1]]
+        nc.vector.tensor_copy(w1_bf[0][:].rearrange("p t m j -> p m t j"), dealt[:, :, 0:2, :])
+        nc.scalar.copy(w1_bf[1][:].rearrange("p t m j -> p m t j"), dealt[:, :, 2:4, :])
         for t in range(PACK):
-            if t == 1:
-                nc.vector.tensor_copy(w1_bf23[:].rearrange("p t m j -> p m t j"), dealt[:, :, 2:4, :])
-            nc.vector.quantize_mx(out=w1_codes[t][:].bitcast(FP8X4), scales=w1_bytes[t][:], in_=sources[t].rearrange("p m j -> p (m j)"))
-            nc.tensor.matmul_mx(out=uu[t][:], lhsT=w1_codes[t][:].bitcast(FP8X4), lhsT_scale=w1_bytes[t][:],
-                                rhs=x_codes[:].bitcast(FP8X4), rhs_scale=x_bytes[:], start=True, stop=True)
-            nc.scalar.activation(heat[t][:, S:], uu[t][:], ACT.Tanh)
-            nc.scalar.activation(heat[t][:, :S], heat[t][:, S:], ACT.Exp, scale=0.8)
+            nc.vector.quantize_mx(out=w1_codes[t][:].bitcast(FP8X4), scales=w1_bytes[t][:], in_=w1_bf[t // 2][:, t % 2].rearrange("p m j -> p (m j)"))
+            pieces = ((0, 0, HALF), (4, HALF, HALF)) if t == 0 else ((t, 0, S),)
+            for b, c0, n in pieces:
+                uu = bank(b, [P, n], f"uu{t}_{c0}")
+                nc.tensor.matmul_mx(out=uu[:], lhsT=w1_codes[t][:].bitcast(FP8X4), lhsT_scale=w1_bytes[t][:],
+                                    rhs=x_codes[:, c0 : c0 + n].bitcast(FP8X4), rhs_scale=x_bytes[:, c0 : c0 + n], start=True, stop=True)
+                nc.scalar.activation(heat[t][:, S + c0 : S + c0 + n], uu[:], ACT.Tanh)
+            for b, c0, n in pieces:
+                nc.scalar.activation(heat[t][:, c0 : c0 + n], heat[t][:, S + c0 : S + c0 + n], ACT.Exp, scale=0.8)
 
         w2_bf = keep.tile([P, N, PACK], BF16, name="w2_bf", align_bytes=64)
         w2_codes = keep.tile([P, N], U32, name="w2_codes", align_bytes=64)
@@ -78,63 +84,67 @@ def tile_picked_yheatg_div_p_kernel(tc, x_words, x_scales, w1, unit, w2, offs, h
         nc.vector.tensor_copy(w2_bf[:], w2_raw[:].rearrange("p j c -> p c j"))
         nc.vector.quantize_mx(out=w2_codes[:].bitcast(FP8X4), scales=w2_bytes[:], in_=w2_bf[:].rearrange("p c j -> p (c j)"))
 
-        grad = [keep.tile([P, 2 * S], F32, name=f"grad{t}") for t in range(PACK)]
-        sq = [keep.tile([P, 2 * S], F32, name=f"sq{t}") for t in range(PACK)]
-        gsum = [keep.tile([P, S], F32, name=f"gsum{t}") for t in range(PACK)]
-        qq = [keep.tile([P, S], F32, name=f"qq{t}") for t in range(PACK)]
+        grad = [[keep.tile([P, S], F32, name=f"grad{t}_{e}") for e in range(2)] for t in range(PACK)]
+        sq = [[keep.tile([P, S], F32, name=f"sq{t}_{e}") for e in range(2)] for t in range(PACK)]
         field = keep.tile([P, PACK, 2 * S], F32, name="field")
         fetched = keep.tile([P, PACK, S], F32, name="fetched")
+        blocks = [slice(b * P, (b + 1) * P) for b in range(S // P)]
 
         def edges(t):
             if t < 2:
                 nc.vector.tensor_copy(heat_copy[t][:], heat[t][:, :S])
             else:
                 nc.sync.dma_start(heat_copy[t][:], heat[t][:, :S])
-            nc.vector.tensor_tensor(grad[t][:, :S], heat[t][:].indirect(h1_t[:]), heat_copy[t][:], ALU.subtract)
-            nc.vector.tensor_tensor(grad[t][:, S:], heat[t][:].indirect(h2_t[:]), heat_copy[t][:], ALU.subtract)
-            nc.scalar.activation(sq[t][:], grad[t][:], ACT.Square)
-
-        def norm(t):
-            nc.vector.tensor_tensor(gsum[t][:], grad[t][:, :S], grad[t][:, S:], ALU.add)
-            nc.vector.tensor_tensor(qq[t][:], sq[t][:, :S], sq[t][:, S:], ALU.add)
-            nc.scalar.activation(field[:, t, S:], qq[t][:], ACT.Abs_reciprocal_sqrt, bias=0.05)
+            for e, lst in enumerate((h1_t, h2_t)):
+                nc.vector.tensor_tensor(grad[t][e][:], heat[t][:].indirect(lst[:]), heat_copy[t][:], ALU.subtract)
 
         def unit_field(t):
-            nc.vector.scalar_tensor_tensor(field[:, t, :S], gsum[t][:], unit_t[:, t : t + 1], field[:, t, S:], ALU.mult, ALU.mult)
+            norm2 = bank(5 - t % 2, [P, S], f"norm2_{t}")
+            for e in range(2):
+                nc.scalar.activation(sq[t][e][:], grad[t][e][:], ACT.Square)
+                for b, cols in enumerate(blocks):
+                    nc.tensor.matmul(norm2[:, cols], sq[t][e][:, cols], ident[:], is_transpose=True, start=(e == 0 and b == 0), stop=(e == 1 and b == len(blocks) - 1))
+            nc.scalar.activation(field[:, t, S:], norm2[:], ACT.Abs_reciprocal_sqrt, bias=0.05)
+            inv = bank(6 + t % 2, [P, S], f"inv{t}")
+            for cols in blocks:
+                nc.tensor.transpose(inv[:, cols], field[:, t, S + cols.start : S + cols.stop], ident[:])
+            both = field[:, t, S:] if t < 2 else grad[t][0][:]
+            nc.vector.tensor_tensor(both, grad[t][0][:], grad[t][1][:], ALU.add)
+            nc.vector.scalar_tensor_tensor(field[:, t, :S], both, unit_t[:, t : t + 1], inv[:], ALU.mult, ALU.mult)
 
         def fetch(t, c0, n):
-            nc.scalar.activation(fetched[:, t, c0 : c0 + n], field[:, t, :].indirect(h3_t[:, c0 // 16 : (c0 + n) // 16]), ACT.Copy)
+            looked_up = field[:, t, :].indirect(h3_t[:, c0 // 16 : (c0 + n) // 16])
+            if t == 3 and c0 == 0:
+                nc.vector.tensor_copy(fetched[:, t, c0 : c0 + n], looked_up)
+            else:
+                nc.scalar.activation(fetched[:, t, c0 : c0 + n], looked_up, ACT.Copy)
 
         edges(0)
         edges(1)
-        norm(0)
-        edges(2)
-        norm(1)
         unit_field(0)
-        fetch(0, 0, S)
-        edges(3)
-        norm(2)
+        edges(2)
         unit_field(1)
-        fetch(1, 0, S)
-        norm(3)
+        edges(3)
         unit_field(2)
-        fetch(2, 0, S)
         unit_field(3)
 
         out_view = out.rearrange("(g p) j -> p g j", p=P)
-        for c0, n in CHUNKS:
+        for k, (c0, n) in enumerate(CHUNKS):
+            if c0 % HALF == 0:
+                for t in range(PACK - 1):
+                    fetch(t, c0, HALF)
             fetch(3, c0, n)
             hid = keep.tile([P, n * PACK], BF16, name=f"hid{c0}", align_bytes=64)
             nc.vector.tensor_tensor(
-                hid[:].rearrange("p (c i t) -> p c t i", i=4, t=PACK),
-                field[:, :, c0 : c0 + n].rearrange("p t (c i) -> p c t i", i=4),
-                fetched[:, :, c0 : c0 + n].rearrange("p t (c i) -> p c t i", i=4),
+                hid[:].rearrange("p (c i t) -> p c t i", i=2, t=PACK),
+                field[:, :, c0 : c0 + n].rearrange("p t (c i) -> p c t i", i=2),
+                fetched[:, :, c0 : c0 + n].rearrange("p t (c i) -> p c t i", i=2),
                 ALU.subtract,
             )
             hid_codes = keep.tile([P, n], U32, name=f"hid_codes{c0}", align_bytes=64)
             hid_bytes = keep.tile([P, n], U8, name=f"hid_bytes{c0}", align_bytes=64)
             nc.vector.quantize_mx(out=hid_codes[:].bitcast(FP8X4), scales=hid_bytes[:], in_=hid[:])
-            acc = psum.tile([P, 2, n], F32, name=f"acc{c0}")
+            acc = bank(k, [P, 2, n], f"acc{c0}")
             for g in range(2):
                 nc.tensor.matmul_mx(out=acc[:, g, :], lhsT=w2_codes[:, g * P : (g + 1) * P].bitcast(FP8X4), lhsT_scale=w2_bytes[:, g * P : (g + 1) * P],
                                     rhs=hid_codes[:].bitcast(FP8X4), rhs_scale=hid_bytes[:], start=True, stop=True)

@@ -19,7 +19,8 @@ ALU = mybir.AluOpType
 P = 128
 PACK = 4
 HALF = S // 2
-CHUNKS = ((0, 128), (128, 128), (256, 128), (384, 128))
+CHUNKS = ((0, 128), (128, 128), (256, 128), (384, 64), (448, 64))
+ROW = S + P
 
 
 def tile_picked_yheatg_div_p_kernel(tc, x_words, x_scales, w1, unit, w2, offs, h1, h2, h3, out):
@@ -33,13 +34,13 @@ def tile_picked_yheatg_div_p_kernel(tc, x_words, x_scales, w1, unit, w2, offs, h
 
         offs_t = keep.tile([P, S // 16], U16, name="offs_t")
         nc.sync.dma_start(offs_t[:], offs)
-        words = keep.tile([P, T], U32, name="words")
-        nc.sync.dma_start(words[:].bitcast(I32), x_words[0].rearrange("p n r -> p (n r)").bitcast(I32))
         scales = keep.tile([P, T], U8, name="scales")
         for q in range(4):
             (nc.scalar if q < 2 else nc.sync).dma_start(scales[32 * q : 32 * q + 32, :].bitcast(I32), x_scales[0, 4 * q : 4 * q + 4, :].bitcast(I32).partition_broadcast(8))
         w1_raw = keep.tile([P, PACK, H], F32, name="w1_raw")
         nc.sync.dma_start(w1_raw[:], w1.rearrange("(p j) c -> p j c", j=PACK))
+        words = keep.tile([P, T], U32, name="words")
+        nc.sync.dma_start(words[:].bitcast(I32), x_words[0].rearrange("p n r -> p (n r)").bitcast(I32))
         w2_raw = keep.tile([P, PACK, N], F32, name="w2_raw")
         nc.sync.dma_start(w2_raw[:], w2.rearrange("(p j) c -> p j c", j=PACK))
         lists = []
@@ -55,8 +56,10 @@ def tile_picked_yheatg_div_p_kernel(tc, x_words, x_scales, w1, unit, w2, offs, h
 
         x_codes = keep.tile([P, S], U32, name="x_codes", align_bytes=64)
         x_bytes = keep.tile([P, S], U8, name="x_bytes", align_bytes=64)
-        nc.vector.tensor_copy(x_codes[:], words[:].indirect(offs_t[:]))
         nc.vector.tensor_copy(x_bytes[:], scales[:].indirect(offs_t[:]))
+        first = ((0, 0, HALF), (4, HALF, P), (5, HALF + P, P))
+        for b, c0, n in first:
+            nc.vector.tensor_copy(x_codes[:, c0 : c0 + n], words[:].indirect(offs_t[:, c0 // 16 : (c0 + n) // 16]))
 
         dealt = w1_raw[:].rearrange("p j (m t) -> p m t j", t=PACK)
         w1_bf = [keep.tile([P, 2, P, PACK], BF16, name=f"w1_bf{u}", align_bytes=64) for u in range(2)]
@@ -69,13 +72,12 @@ def tile_picked_yheatg_div_p_kernel(tc, x_words, x_scales, w1, unit, w2, offs, h
         nc.scalar.copy(w1_bf[1][:].rearrange("p t m j -> p m t j"), dealt[:, :, 2:4, :])
         for t in range(PACK):
             nc.vector.quantize_mx(out=w1_codes[t][:].bitcast(FP8X4), scales=w1_bytes[t][:], in_=w1_bf[t // 2][:, t % 2].rearrange("p m j -> p (m j)"))
-            pieces = ((0, 0, HALF), (4, HALF, HALF)) if t == 0 else ((t, 0, S),)
+            pieces = first if t == 0 else ((t, 0, S),)
             for b, c0, n in pieces:
                 uu = bank(b, [P, n], f"uu{t}_{c0}")
                 nc.tensor.matmul_mx(out=uu[:], lhsT=w1_codes[t][:].bitcast(FP8X4), lhsT_scale=w1_bytes[t][:],
                                     rhs=x_codes[:, c0 : c0 + n].bitcast(FP8X4), rhs_scale=x_bytes[:, c0 : c0 + n], start=True, stop=True)
                 nc.scalar.activation(heat[t][:, S + c0 : S + c0 + n], uu[:], ACT.Tanh)
-            for b, c0, n in pieces:
                 nc.scalar.activation(heat[t][:, c0 : c0 + n], heat[t][:, S + c0 : S + c0 + n], ACT.Exp, scale=0.8)
 
         w2_bf = keep.tile([P, N, PACK], BF16, name="w2_bf", align_bytes=64)
@@ -86,68 +88,99 @@ def tile_picked_yheatg_div_p_kernel(tc, x_words, x_scales, w1, unit, w2, offs, h
 
         grad = [[keep.tile([P, S], F32, name=f"grad{t}_{e}") for e in range(2)] for t in range(PACK)]
         sq = [[keep.tile([P, S], F32, name=f"sq{t}_{e}") for e in range(2)] for t in range(PACK)]
-        field = keep.tile([P, PACK, 2 * S], F32, name="field")
-        fetched = keep.tile([P, PACK, S], F32, name="fetched")
+        field = keep.tile([P, PACK * ROW], F32, name="field")
+        planes = field[:].rearrange("p (t c) -> p t c", t=PACK)
+        turned = [keep.tile([P, S // P, P], F32, name=f"turned{t}") for t in range(PACK - 1)]
+        fetched = [keep.tile([P, PACK, HALF], F32, name=f"fetched{u}") for u in range(2)]
         blocks = [slice(b * P, (b + 1) * P) for b in range(S // P)]
 
+        def pieces(t):
+            return ((0, HALF), (HALF, HALF)) if t == PACK - 1 else ((0, S),)
+
         def edges(t):
-            if t < 2:
+            if t == 0:
+                for c0, n in ((0, HALF + P), (HALF + P, P)):
+                    nc.vector.tensor_copy(heat_copy[t][:, c0 : c0 + n], heat[t][:, c0 : c0 + n])
+            elif t == 1:
                 nc.vector.tensor_copy(heat_copy[t][:], heat[t][:, :S])
             else:
                 nc.sync.dma_start(heat_copy[t][:], heat[t][:, :S])
-            for e, lst in enumerate((h1_t, h2_t)):
-                nc.vector.tensor_tensor(grad[t][e][:], heat[t][:].indirect(lst[:]), heat_copy[t][:], ALU.subtract)
+            nc.vector.tensor_tensor(grad[t][0][:], heat[t][:].indirect(h1_t[:]), heat_copy[t][:], ALU.subtract)
+            for c0, n in pieces(t):
+                nc.vector.tensor_tensor(grad[t][1][:, c0 : c0 + n], heat[t][:].indirect(h2_t[:, c0 // 16 : (c0 + n) // 16]), heat_copy[t][:, c0 : c0 + n], ALU.subtract)
+
+        norm2 = {}
+
+        def squares(t):
+            nc.scalar.activation(sq[t][0][:], grad[t][0][:], ACT.Square)
+            for c0, n in pieces(t):
+                norm2[t, c0] = bank((5, 4, 5, 3)[t] if c0 == 0 else 4, [P, n], f"norm2_{t}_{c0}")
+                for b in range(n // P):
+                    nc.tensor.matmul(norm2[t, c0][:, blocks[b]], sq[t][0][:, c0 + b * P : c0 + (b + 1) * P], ident[:], is_transpose=True, start=(b == 0), stop=False)
+            for c0, n in pieces(t):
+                nc.scalar.activation(sq[t][1][:, c0 : c0 + n], grad[t][1][:, c0 : c0 + n], ACT.Square)
+                for b in range(n // P):
+                    nc.tensor.matmul(norm2[t, c0][:, blocks[b]], sq[t][1][:, c0 + b * P : c0 + (b + 1) * P], ident[:], is_transpose=True, start=False, stop=(b == n // P - 1))
 
         def unit_field(t):
-            norm2 = bank(5 - t % 2, [P, S], f"norm2_{t}")
-            for e in range(2):
-                nc.scalar.activation(sq[t][e][:], grad[t][e][:], ACT.Square)
-                for b, cols in enumerate(blocks):
-                    nc.tensor.matmul(norm2[:, cols], sq[t][e][:, cols], ident[:], is_transpose=True, start=(e == 0 and b == 0), stop=(e == 1 and b == len(blocks) - 1))
-            nc.scalar.activation(field[:, t, S:], norm2[:], ACT.Abs_reciprocal_sqrt, bias=0.05)
             inv = bank(6 + t % 2, [P, S], f"inv{t}")
-            for cols in blocks:
-                nc.tensor.transpose(inv[:, cols], field[:, t, S + cols.start : S + cols.stop], ident[:])
-            both = field[:, t, S:] if t < 2 else grad[t][0][:]
+            for c0, n in pieces(t):
+                if t < PACK - 1:
+                    inv_t = turned[t][:]
+                else:
+                    inv_t = planes[:, 0:4:3, S:] if c0 == 0 else planes[:, 1:3, S:]
+                nc.scalar.activation(inv_t, norm2[t, c0][:].rearrange("p (b c) -> p b c", c=P), ACT.Abs_reciprocal_sqrt, bias=0.05)
+                for b in range(n // P):
+                    nc.tensor.transpose(inv[:, c0 + b * P : c0 + (b + 1) * P], inv_t[:, b, :], ident[:])
+            both = turned[t][:].rearrange("p b c -> p (b c)") if t < 2 else grad[t][0][:]
             nc.vector.tensor_tensor(both, grad[t][0][:], grad[t][1][:], ALU.add)
-            nc.vector.scalar_tensor_tensor(field[:, t, :S], both, unit_t[:, t : t + 1], inv[:], ALU.mult, ALU.mult)
+            nc.vector.scalar_tensor_tensor(planes[:, t, :S], both, unit_t[:, t : t + 1], inv[:], ALU.mult, ALU.mult)
 
-        def fetch(t, c0, n):
-            looked_up = field[:, t, :].indirect(h3_t[:, c0 // 16 : (c0 + n) // 16])
+        def fetch(t, c0, n, end):
+            looked_up = field[:, t * ROW : end].indirect(h3_t[:, c0 // 16 : (c0 + n) // 16])
             if t == 3 and c0 == 0:
-                nc.vector.tensor_copy(fetched[:, t, c0 : c0 + n], looked_up)
+                nc.vector.tensor_copy(fetched[c0 // HALF][:, t, c0 % HALF : c0 % HALF + n], looked_up)
             else:
-                nc.scalar.activation(fetched[:, t, c0 : c0 + n], looked_up, ACT.Copy)
+                nc.scalar.activation(fetched[c0 // HALF][:, t, c0 % HALF : c0 % HALF + n], looked_up, ACT.Copy)
 
-        edges(0)
-        edges(1)
-        unit_field(0)
-        edges(2)
-        unit_field(1)
-        edges(3)
-        unit_field(2)
-        unit_field(3)
+        for t in range(PACK):
+            edges(t)
+        for pair in ((0, 1), (2, 3)):
+            for t in pair:
+                squares(t)
+            for t in pair:
+                unit_field(t)
 
         out_view = out.rearrange("(g p) j -> p g j", p=P)
+        accs = []
         for k, (c0, n) in enumerate(CHUNKS):
-            if c0 % HALF == 0:
-                for t in range(PACK - 1):
-                    fetch(t, c0, HALF)
-            fetch(3, c0, n)
+            if c0 == 0:
+                fetch(0, 0, HALF, S)
+                fetch(1, 0, HALF, 2 * ROW)
+                fetch(2, 0, HALF, 3 * ROW)
+                fetch(0, HALF, HALF, 2 * ROW)
+                fetch(3, 0, P, 3 * ROW + S)
+                fetch(3, P, P, 3 * ROW + S)
+            if c0 == HALF:
+                fetch(1, HALF, HALF, 3 * ROW + 16)
+                fetch(2, HALF, HALF, 3 * ROW + 16)
+                fetch(3, HALF, HALF, 3 * ROW + S)
             hid = keep.tile([P, n * PACK], BF16, name=f"hid{c0}", align_bytes=64)
             nc.vector.tensor_tensor(
                 hid[:].rearrange("p (c i t) -> p c t i", i=2, t=PACK),
-                field[:, :, c0 : c0 + n].rearrange("p t (c i) -> p c t i", i=2),
-                fetched[:, :, c0 : c0 + n].rearrange("p t (c i) -> p c t i", i=2),
+                planes[:, :, c0 : c0 + n].rearrange("p t (c i) -> p c t i", i=2),
+                fetched[c0 // HALF][:, :, c0 % HALF : c0 % HALF + n].rearrange("p t (c i) -> p c t i", i=2),
                 ALU.subtract,
             )
             hid_codes = keep.tile([P, n], U32, name=f"hid_codes{c0}", align_bytes=64)
             hid_bytes = keep.tile([P, n], U8, name=f"hid_bytes{c0}", align_bytes=64)
             nc.vector.quantize_mx(out=hid_codes[:].bitcast(FP8X4), scales=hid_bytes[:], in_=hid[:])
             acc = bank(k, [P, 2, n], f"acc{c0}")
+            accs.append(acc)
             for g in range(2):
                 nc.tensor.matmul_mx(out=acc[:, g, :], lhsT=w2_codes[:, g * P : (g + 1) * P].bitcast(FP8X4), lhsT_scale=w2_bytes[:, g * P : (g + 1) * P],
                                     rhs=hid_codes[:].bitcast(FP8X4), rhs_scale=hid_bytes[:], start=True, stop=True)
+        for acc, (c0, n) in zip(accs, CHUNKS):
             staged = keep.tile([P, 2, n], F32, name=f"staged{c0}")
             nc.scalar.copy(staged[:], acc[:])
             nc.sync.dma_start(out_view[:, :, c0 : c0 + n], staged[:])

from contextlib import ExitStack

import concourse.mybir as mybir
from concourse.masks import make_identity

K, T, S, N, H = 512, 1024, 512, 256, 512
FLOPS = 2 * K * H * S + 2 * H * N * S

F32 = mybir.dt.float32
BF16 = mybir.dt.bfloat16
I32 = mybir.dt.int32
U32 = mybir.dt.uint32
U16 = mybir.dt.uint16
U8 = mybir.dt.uint8
FP8X4 = mybir.dt.float8_e4m3fn_x4
ACT = mybir.ActivationFunctionType
ALU = mybir.AluOpType

P = 128
PACK = 4
HALF = S // 2
CHUNKS = ((0, 128), (128, 128), (256, 128), (384, 64), (448, 64))
ROW = S + P


def tile_picked_yheatg_div_p_kernel(tc, x_words, x_scales, w1, unit, w2, offs, h1, h2, h3, out):
    nc = tc.nc
    with ExitStack() as ctx:
        keep = ctx.enter_context(tc.tile_pool(name="keep", bufs=1))
        psum = ctx.enter_context(tc.psum_pool(name="psum", bufs=1))

        def bank(number, shape, name):
            return psum.tile(shape, F32, name=name, tag=f"bank{number}")

        offs_t = keep.tile([P, S // 16], U16, name="offs_t")
        nc.sync.dma_start(offs_t[:], offs)
        scales = keep.tile([P, T], U8, name="scales")
        for q in range(4):
            (nc.scalar if q < 2 else nc.sync).dma_start(scales[32 * q : 32 * q + 32, :].bitcast(I32), x_scales[0, 4 * q : 4 * q + 4, :].bitcast(I32).partition_broadcast(8))
        w1_raw = keep.tile([P, PACK, H], F32, name="w1_raw")
        nc.sync.dma_start(w1_raw[:], w1.rearrange("(p j) c -> p j c", j=PACK))
        words = keep.tile([P, T], U32, name="words")
        nc.sync.dma_start(words[:].bitcast(I32), x_words[0].rearrange("p n r -> p (n r)").bitcast(I32))
        w2_raw = keep.tile([P, PACK, N], F32, name="w2_raw")
        nc.sync.dma_start(w2_raw[:], w2.rearrange("(p j) c -> p j c", j=PACK))
        lists = []
        for name, src in (("h1_t", h1), ("h2_t", h2), ("h3_t", h3)):
            lst = keep.tile([P, S // 16], U16, name=name)
            nc.sync.dma_start(lst[:], src)
            lists.append(lst)
        h1_t, h2_t, h3_t = lists
        unit_t = keep.tile([P, PACK], F32, name="unit_t")
        nc.sync.dma_start(unit_t[:], unit.rearrange("(p t) o -> p (t o)", t=PACK))
        ident = keep.tile([P, P], F32, name="ident")
        make_identity(nc, ident[:])

        x_codes = keep.tile([P, S], U32, name="x_codes", align_bytes=64)
        x_bytes = keep.tile([P, S], U8, name="x_bytes", align_bytes=64)
        nc.vector.tensor_copy(x_bytes[:], scales[:].indirect(offs_t[:]))
        first = ((0, 0, HALF), (4, HALF, P), (5, HALF + P, P))
        for b, c0, n in first:
            nc.vector.tensor_copy(x_codes[:, c0 : c0 + n], words[:].indirect(offs_t[:, c0 // 16 : (c0 + n) // 16]))

        dealt = w1_raw[:].rearrange("p j (m t) -> p m t j", t=PACK)
        w1_bf = [keep.tile([P, 2, P, PACK], BF16, name=f"w1_bf{u}", align_bytes=64) for u in range(2)]
        w1_codes = [keep.tile([P, P], U32, name=f"w1_codes{t}", align_bytes=64) for t in range(PACK)]
        w1_bytes = [keep.tile([P, P], U8, name=f"w1_bytes{t}", align_bytes=64) for t in range(PACK)]
        heat = [keep.tile([P, 2 * S], F32, name=f"heat{t}") for t in range(PACK)]
        heat_copy = [keep.tile([P, S], F32, name=f"heat_copy{t}") for t in range(PACK)]

        nc.vector.tensor_copy(w1_bf[0][:].rearrange("p t m j -> p m t j"), dealt[:, :, 0:2, :])
        nc.scalar.copy(w1_bf[1][:].rearrange("p t m j -> p m t j"), dealt[:, :, 2:4, :])
        for t in range(PACK):
            nc.vector.quantize_mx(out=w1_codes[t][:].bitcast(FP8X4), scales=w1_bytes[t][:], in_=w1_bf[t // 2][:, t % 2].rearrange("p m j -> p (m j)"))
            pieces = first if t == 0 else ((t, 0, S),)
            for b, c0, n in pieces:
                uu = bank(b, [P, n], f"uu{t}_{c0}")
                nc.tensor.matmul_mx(out=uu[:], lhsT=w1_codes[t][:].bitcast(FP8X4), lhsT_scale=w1_bytes[t][:],
                                    rhs=x_codes[:, c0 : c0 + n].bitcast(FP8X4), rhs_scale=x_bytes[:, c0 : c0 + n], start=True, stop=True)
                nc.scalar.activation(heat[t][:, S + c0 : S + c0 + n], uu[:], ACT.Tanh)
                nc.scalar.activation(heat[t][:, c0 : c0 + n], heat[t][:, S + c0 : S + c0 + n], ACT.Exp, scale=0.8)

        w2_bf = keep.tile([P, N, PACK], BF16, name="w2_bf", align_bytes=64)
        w2_codes = keep.tile([P, N], U32, name="w2_codes", align_bytes=64)
        w2_bytes = keep.tile([P, N], U8, name="w2_bytes", align_bytes=64)
        nc.vector.tensor_copy(w2_bf[:], w2_raw[:].rearrange("p j c -> p c j"))
        nc.vector.quantize_mx(out=w2_codes[:].bitcast(FP8X4), scales=w2_bytes[:], in_=w2_bf[:].rearrange("p c j -> p (c j)"))

        grad = [[keep.tile([P, S], F32, name=f"grad{t}_{e}") for e in range(2)] for t in range(PACK)]
        sq = [[keep.tile([P, S], F32, name=f"sq{t}_{e}") for e in range(2)] for t in range(PACK)]
        field = keep.tile([P, PACK * ROW], F32, name="field")
        planes = field[:].rearrange("p (t c) -> p t c", t=PACK)
        turned = [keep.tile([P, S // P, P], F32, name=f"turned{t}") for t in range(PACK - 1)]
        fetched = [keep.tile([P, PACK, HALF], F32, name=f"fetched{u}") for u in range(2)]
        blocks = [slice(b * P, (b + 1) * P) for b in range(S // P)]

        def pieces(t):
            return ((0, HALF), (HALF, HALF)) if t == PACK - 1 else ((0, S),)

        def edges(t):
            if t == 0:
                for c0, n in ((0, HALF + P), (HALF + P, P)):
                    nc.vector.tensor_copy(heat_copy[t][:, c0 : c0 + n], heat[t][:, c0 : c0 + n])
            elif t == 1:
                nc.vector.tensor_copy(heat_copy[t][:], heat[t][:, :S])
            else:
                nc.sync.dma_start(heat_copy[t][:], heat[t][:, :S])
            nc.vector.tensor_tensor(grad[t][0][:], heat[t][:].indirect(h1_t[:]), heat_copy[t][:], ALU.subtract)
            for c0, n in pieces(t):
                nc.vector.tensor_tensor(grad[t][1][:, c0 : c0 + n], heat[t][:].indirect(h2_t[:, c0 // 16 : (c0 + n) // 16]), heat_copy[t][:, c0 : c0 + n], ALU.subtract)

        norm2 = {}

        def squares(t):
            nc.scalar.activation(sq[t][0][:], grad[t][0][:], ACT.Square)
            for c0, n in pieces(t):
                norm2[t, c0] = bank((5, 4, 5, 3)[t] if c0 == 0 else 4, [P, n], f"norm2_{t}_{c0}")
                for b in range(n // P):
                    nc.tensor.matmul(norm2[t, c0][:, blocks[b]], sq[t][0][:, c0 + b * P : c0 + (b + 1) * P], ident[:], is_transpose=True, start=(b == 0), stop=False)
            for c0, n in pieces(t):
                nc.scalar.activation(sq[t][1][:, c0 : c0 + n], grad[t][1][:, c0 : c0 + n], ACT.Square)
                for b in range(n // P):
                    nc.tensor.matmul(norm2[t, c0][:, blocks[b]], sq[t][1][:, c0 + b * P : c0 + (b + 1) * P], ident[:], is_transpose=True, start=False, stop=(b == n // P - 1))

        def unit_field(t):
            inv = bank(6 + t % 2, [P, S], f"inv{t}")
            for c0, n in pieces(t):
                if t < PACK - 1:
                    inv_t = turned[t][:]
                else:
                    inv_t = planes[:, 0:4:3, S:] if c0 == 0 else planes[:, 1:3, S:]
                nc.scalar.activation(inv_t, norm2[t, c0][:].rearrange("p (b c) -> p b c", c=P), ACT.Abs_reciprocal_sqrt, bias=0.05)
                for b in range(n // P):
                    nc.tensor.transpose(inv[:, c0 + b * P : c0 + (b + 1) * P], inv_t[:, b, :], ident[:])
            both = turned[t][:].rearrange("p b c -> p (b c)") if t < 2 else grad[t][0][:]
            nc.vector.tensor_tensor(both, grad[t][0][:], grad[t][1][:], ALU.add)
            nc.vector.scalar_tensor_tensor(planes[:, t, :S], both, unit_t[:, t : t + 1], inv[:], ALU.mult, ALU.mult)

        def fetch(t, c0, n, end):
            looked_up = field[:, t * ROW : end].indirect(h3_t[:, c0 // 16 : (c0 + n) // 16])
            if t == 3 and c0 == 0:
                nc.vector.tensor_copy(fetched[c0 // HALF][:, t, c0 % HALF : c0 % HALF + n], looked_up)
            else:
                nc.scalar.activation(fetched[c0 // HALF][:, t, c0 % HALF : c0 % HALF + n], looked_up, ACT.Copy)

        for t in range(PACK):
            edges(t)
        for pair in ((0, 1), (2, 3)):
            for t in pair:
                squares(t)
            for t in pair:
                unit_field(t)

        out_view = out.rearrange("(g p) j -> p g j", p=P)
        accs = []
        for k, (c0, n) in enumerate(CHUNKS):
            if c0 == 0:
                fetch(0, 0, HALF, S)
                fetch(1, 0, HALF, 2 * ROW)
                fetch(2, 0, HALF, 3 * ROW)
                fetch(0, HALF, HALF, 2 * ROW)
                fetch(3, 0, P, 3 * ROW + S)
                fetch(3, P, P, 3 * ROW + S)
            if c0 == HALF:
                fetch(1, HALF, HALF, 3 * ROW + 16)
                fetch(2, HALF, HALF, 3 * ROW + 16)
                fetch(3, HALF, HALF, 3 * ROW + S)
            hid = keep.tile([P, n * PACK], BF16, name=f"hid{c0}", align_bytes=64)
            nc.vector.tensor_tensor(
                hid[:].rearrange("p (c i t) -> p c t i", i=2, t=PACK),
                planes[:, :, c0 : c0 + n].rearrange("p t (c i) -> p c t i", i=2),
                fetched[c0 // HALF][:, :, c0 % HALF : c0 % HALF + n].rearrange("p t (c i) -> p c t i", i=2),
                ALU.subtract,
            )
            hid_codes = keep.tile([P, n], U32, name=f"hid_codes{c0}", align_bytes=64)
            hid_bytes = keep.tile([P, n], U8, name=f"hid_bytes{c0}", align_bytes=64)
            nc.vector.quantize_mx(out=hid_codes[:].bitcast(FP8X4), scales=hid_bytes[:], in_=hid[:])
            acc = bank(k, [P, 2, n], f"acc{c0}")
            accs.append(acc)
            for g in range(2):
                nc.tensor.matmul_mx(out=acc[:, g, :], lhsT=w2_codes[:, g * P : (g + 1) * P].bitcast(FP8X4), lhsT_scale=w2_bytes[:, g * P : (g + 1) * P],
                                    rhs=hid_codes[:].bitcast(FP8X4), rhs_scale=hid_bytes[:], start=True, stop=True)
        for acc, (c0, n) in zip(accs, CHUNKS):
            staged = keep.tile([P, 2, n], F32, name=f"staged{c0}")
            nc.scalar.copy(staged[:], acc[:])
            nc.sync.dma_start(out_view[:, :, c0 : c0 + n], staged[:])
